import numpy as np, ml_dtypes
CORES = [1,3,5,9,11,13]
N = 6
import mx_ref
NC, ROOT = 384, 4
BF = ml_dtypes.bfloat16
def cut(t, i, w=512):
    return t[:, w * i:w * i + w]
def term(a, B):
    return np.stack([np.maximum(mx_ref.matmul(mx_ref.quantize(cut(a, i)), B), 0) for i in range(4)], axis=2).reshape(128, -1)
def setup_inputs(rng):
    def f(*shape):
        return mx_ref.flush((rng.standard_normal(shape, dtype=np.float32) * np.exp2(rng.integers(-2, 3, shape[:-1] + (1,)))).astype(BF))
    return {"a": f(N, 128, 4 * 512), "b": f(N, 128, 4 * NC)}
def setup_inputs_blocks(rng):
    d = setup_inputs(rng)
    for k in ("a", "b"): d[k] = mx_ref.spread(d[k], rng, 2)
    return d
def setup_inputs_wide(rng):
    d = setup_inputs(rng)
    for k in ("a", "b"): d[k] = mx_ref.flush((d[k].astype(np.float32) * np.exp2(rng.integers(-4, 5, (N, 1, 1))).astype(np.float32)).astype(BF))
    return d
def setup_inputs_lossless(rng):
    a = np.zeros((N, 128, 4 * 128, 4), np.float32)
    for r in range(N):
        k = rng.integers(0, 512, size=4 * 128)
        a[r, k // 4, np.arange(4 * 128), k % 4] = 1.0
    size = np.repeat(2.0 ** rng.integers(-4, 5, size=(1, 1, (4 * NC) // 4)), 4, axis=2)
    b = (rng.random((N, 128, 4 * NC)) < 0.8) * size
    return {"a": a.reshape(N, 128, 4 * 512).astype(BF), "b": b.astype(np.float32).astype(BF)}
def reference(a, b):
    B0 = mx_ref.quantize(b[ROOT])
    T = [term(a[r], B0) for r in range(N)]
    y = np.zeros((N, 128, 4 * NC), np.float32)
    y[:] = mx_ref.total(T)
    return {"y": y}

@@ -1,0 +1,235 @@
+from concourse.bass import DstId, RemoteDMATransfer
+from concourse.mybir import dt, AluOpType, ActivationFunctionType
+
+SIM_CORES = 16
+NC = 384
+HALVES = 2
+HC = NC // HALVES
+PER = 3
+P = 4
+MT = 128
+BANK = 512
+SELW = 4 * MT + P - 1
+
+SCRATCH = {
+    "b_in": ("sbuf", [128, 4 * NC], "bfloat16"),
+    "a_in": ("sbuf", [128, 4 * 4 * MT], "bfloat16"),
+    "qb": ("sbuf", [128, NC], "float8_e4m3fn_x4"),
+    "pb": ("sbuf", [128, NC], "uint8"),
+    "qa": ("sbuf", [128, P * MT], "float8_e4m3fn_x4"),
+    "pa": ("sbuf", [128, P * MT], "uint8"),
+    "lqb": ("sbuf", [128, HC], "float8_e4m3fn_x4"),
+    "lpb": ("sbuf", [128, HC], "uint8"),
+    "u": ("sbuf", [128, PER * P * HC], "bfloat16"),
+    "t": ("sbuf", [128, P * HC], "bfloat16"),
+    "h": ("sbuf", [128, 4 * HC], "bfloat16"),
+    "qh": ("sbuf", [128, HC], "float8_e4m3fn_x4"),
+    "ph": ("sbuf", [128, HC], "uint8"),
+    "ones": ("sbuf", [128, SELW], "bfloat16"),
+    "strip": ("sbuf", [128, SELW], "bfloat16"),
+    "qw": ("sbuf", [128, P * MT], "float8_e4m3fn_x4"),
+    "pw": ("sbuf", [128, P * MT], "uint8"),
+    "yt": ("sbuf", [128, 4 * NC], "float32"),
+    "ps": ("psum", [128, BANK * 8], "float32"),
+}
+for _k in range(PER):
+    SCRATCH["lqa%d" % _k] = ("sbuf", [128, P * MT], "float8_e4m3fn_x4")
+    SCRATCH["lpa%d" % _k] = ("sbuf", [128, P * MT], "uint8")
+for _k in ("own", "far"):
+    SCRATCH["lqs_" + _k] = ("sbuf", [128, NC], "float8_e4m3fn_x4")
+    SCRATCH["lps_" + _k] = ("sbuf", [128, NC], "uint8")
+
+SEMAPHORES = (["ldb0", "ldb1", "lda0", "lda1", "qub", "qua", "one", "strip", "sel", "sent", "arrb", "mm", "rls", "rlv", "add", "quh",
+               "mmy", "yv", "ys", "st"] + ["arra%d" % k for k in range(PER)]
+              + ["arrs_%s%d" % (w, h) for w in ("own", "far") for h in range(HALVES)])
+
+
+def _engines(mask):
+    return [e for e in range(mask.bit_length()) if mask >> e & 1]
+
+
+def _mask(engines):
+    return sum(1 << e for e in engines)
+
+
+def _plan(T, topo):
+    chips = sorted({topo.chip(c) for c in T.cores})
+    root = T.cores[T.root]
+    members = {ch: sorted([c for c in T.cores if topo.chip(c) == ch], key=lambda c: (c == root, c)) for ch in chips}
+    summers = {}
+    for ch in chips:
+        far = [c for c in T.cores if topo.chip(c) != ch]
+        by_die = {}
+        for c in range(SIM_CORES):
+            if topo.chip(c) == ch and T.rank_of(c) is None and all(topo.may_write(c, f) for f in far):
+                by_die.setdefault(topo.die(c), c)
+        summers[ch] = [by_die[d] for d in sorted(by_die)]
+    return chips, root, members, summers
+
+
+def _dst(topo, c):
+    rid, pid, _ = topo.addr(c)
+    return DstId(rid=rid, pnc=pid)
+
+
+def _send(g, T, topo, sent, parts):
+    g.remote_dma_fused(
+        [RemoteDMATransfer(dst_ids=[_dst(topo, c) for c, _ in dsts], dma_engine_mask=m, remote_sem=sem, srcs=[src], dsts=[d for _, d in dsts])
+         for src, dsts, m, sem in parts], local_sem=T.sem.sent)
+    sent[0] += sum(len(_engines(m)) for _, _, m, _ in parts)
+
+
+def _codes(view):
+    return view.bitcast(dt.uint8)
+
+
+def _half(t, h):
+    return t[:, HC * h:HC * (h + 1)]
+
+
+def _rank(g, core, T, topo, plan):
+    chips, root, members, summers = plan
+    my = topo.chip(core)
+    is_root = core == root
+    sent = [0]
+    queues = (g.sync, g.scalar)
+    if is_root:
+        for h in range(HALVES):
+            queues[h].dma_start(T.b_in[:, 4 * HC * h:4 * HC * (h + 1)], T.b[:, 4 * HC * h:4 * HC * (h + 1)]).then_inc(T.sem["ldb%d" % h], 16)
+    w = 2 * 4 * MT
+    for h in range(2):
+        queues[h].dma_start(T.a_in[:, w * h:w * (h + 1)], T.a[:, w * h:w * (h + 1)]).then_inc(T.sem["lda%d" % h], 16)
+    v = g.vector
+    v.memset(T.ones[:], 1.0).then_inc(T.sem.one, 1)
+    if is_root:
+        for h in range(HALVES):
+            v.wait_ge(T.sem["ldb%d" % h], 16)
+            v.quantize_mx(_half(T.qb, h), _half(T.pb, h), T.b_in[:, 4 * HC * h:4 * HC * (h + 1)]).then_inc(T.sem.qub, 1)
+    for h in range(2):
+        v.wait_ge(T.sem["lda%d" % h], 16)
+        v.quantize_mx(T.qa[:, 2 * MT * h:2 * MT * (h + 1)], T.pa[:, 2 * MT * h:2 * MT * (h + 1)], T.a_in[:, w * h:w * (h + 1)]).then_inc(T.sem.qua, 1)
+    mine = summers[my]
+    on = topo.mask(core, mine[0])
+    if is_root:
+        g.wait_ge(T.sem.qub, HALVES)
+        order = [ch for ch in chips if ch != my] + [my]
+        off = topo.mask(core, summers[order[0]][0])
+        for ch in order:
+            eng = _engines(off if ch != my else on & ~off)
+            k = len(eng) // HALVES
+            ms = [_mask(eng[k * h:k * (h + 1)]) for h in range(HALVES)]
+            for src, dst, f in ((T.qb, T.lqb, _codes), (T.pb, T.lpb, lambda x: x)):
+                _send(g, T, topo, sent, [(f(_half(src, h)), [(summers[ch][h], f(dst[:]))], ms[h], T.sem.arrb) for h in range(HALVES)])
+    g.wait_ge(T.sem.qua, 2)
+    k = members[my].index(core)
+    _send(g, T, topo, sent, [(_codes(T.qa[:]), [(c, _codes(T["lqa%d" % k][:])) for c in mine], on, T.sem["arra%d" % k])])
+    _send(g, T, topo, sent, [(T.pa[:], [(c, T["lpa%d" % k][:]) for c in mine], on, T.sem["arra%d" % k])])
+    g.wait_ge(T.sem.one, 1)
+    g.affine_select(T.strip[:], T.ones[:], [[1, SELW]], AluOpType.is_equal, 0.0, -(P - 1), -P).then_inc(T.sem.strip, 1)
+    v.wait_ge(T.sem.strip, 1)
+    for b in range(P):
+        v.quantize_mx(T.qw[:, MT * b:MT * (b + 1)], T.pw[:, MT * b:MT * (b + 1)], T.strip[:, P - 1 - b:P - 1 - b + 4 * MT]).then_inc(T.sem.sel, 1)
+    te = g.tensor
+    te.wait_ge(T.sem.sel, P)
+    for wch, first in (("own", True), ("far", False)):
+        for h in range(HALVES):
+            te.wait_ge(T.sem["arrs_%s%d" % (wch, h)], _sum_count(topo, summers, my, wch, core, h))
+            for b in range(P):
+                bank = P * h + b
+                m = te.matmul_mx(T.ps[:, BANK * bank:BANK * bank + HC], T.qw[:, MT * b:MT * (b + 1)], T.pw[:, MT * b:MT * (b + 1)],
+                                 _half(T["lqs_" + wch], h), _half(T["lps_" + wch], h), first, not first)
+                if not first:
+                    m.then_inc(T.sem.mmy, 1)
+    for h in range(HALVES):
+        for b in range(P):
+            bank = P * h + b
+            src = T.ps[:, BANK * bank:BANK * bank + HC]
+            out = T.yt[:, 4 * HC * h + b:4 * HC * (h + 1):P]
+            if b % 2 == 0:
+                g.scalar.wait_ge(T.sem.mmy, bank + 1)
+                g.scalar.activation(out, src, ActivationFunctionType.Copy).then_inc(T.sem.ys, 1)
+            else:
+                v.wait_ge(T.sem.mmy, bank + 1)
+                v.tensor_copy(out, src).then_inc(T.sem.yv, 1)
+        g.sync.wait_ge(T.sem.ys, (P // 2) * (h + 1))
+        g.sync.wait_ge(T.sem.yv, (P // 2) * (h + 1))
+        g.sync.dma_start(T.y[:, 4 * HC * h:4 * HC * (h + 1)], T.yt[:, 4 * HC * h:4 * HC * (h + 1)]).then_inc(T.sem.st, 16)
+    g.sync.wait_ge(T.sem.st, 16 * HALVES)
+    g.wait_ge(T.sem.sent, sent[0])
+
+
+def _sum_masks(topo, summers, core, far_core, near_core):
+    off = topo.mask(core, far_core)
+    return off, topo.mask(core, near_core) & ~off
+
+
+def _sum_count(topo, summers, my, wch, core, h):
+    other = [ch for ch in summers if ch != my][0]
+    if wch == "own":
+        s = summers[my][h]
+        off, on = _sum_masks(topo, summers, s, summers[other][h], core)
+        return 2 * len(_engines(on))
+    return 2 * len(_engines(topo.mask(summers[other][h], core)))
+
+
+def _summer(g, core, T, topo, plan):
+    chips, root, members, summers = plan
+    my = topo.chip(core)
+    other = [ch for ch in chips if ch != my][0]
+    half = summers[my].index(core)
+    rchip = topo.chip(root)
+    sent = [0]
+    te, v, sc = g.tensor, g.vector, g.scalar
+    off = topo.mask(root, summers[[ch for ch in chips if ch != rchip][0]][0])
+    nb = len(_engines(off if my != rchip else topo.mask(root, core) & ~off)) // HALVES
+    on_vec = [k for k in range(PER * P) if k in (1, 3)]
+    def clamped_before(k, vec):
+        return len([j for j in range(k) if (j in on_vec) == vec])
+    def z(k):
+        return T.ps[:, BANK * (k % 8):BANK * (k % 8) + HC]
+    def u(k):
+        return T.u[:, HC * k:HC * (k + 1)]
+    te.wait_ge(T.sem.arrb, 2 * nb)
+    for k in range(PER * P):
+        r, i = divmod(k, P)
+        if i == 0:
+            te.wait_ge(T.sem["arra%d" % r], 2 * len(_engines(topo.mask(members[my][r], core))))
+        if k >= 8:
+            j = k - 8
+            te.wait_ge(T.sem.rlv if j in on_vec else T.sem.rls, clamped_before(j + 1, j in on_vec))
+        te.matmul_mx(z(k), T["lqa%d" % r][:, MT * i:MT * (i + 1)], T["lpa%d" % r][:, MT * i:MT * (i + 1)], T.lqb[:], T.lpb[:], True, True).then_inc(T.sem.mm, 1)
+    for k in range(PER * P):
+        if k in on_vec:
+            v.wait_ge(T.sem.mm, k + 1)
+            v.tensor_scalar(u(k), z(k), 0.0, None, AluOpType.max).then_inc(T.sem.rlv, 1)
+        else:
+            sc.wait_ge(T.sem.mm, k + 1)
+            sc.activation(u(k), z(k), ActivationFunctionType.Relu).then_inc(T.sem.rls, 1)
+    v.wait_ge(T.sem.rlv, len(on_vec))
+    for r in range(1, PER):
+        for i in range(P):
+            k = P * r + i
+            v.wait_ge(T.sem.rls, clamped_before(k + 1, False))
+            if r == 1:
+                a, out = u(i), T.t[:, HC * i:HC * (i + 1)]
+            else:
+                v.wait_ge(T.sem.add, i + 1)
+                a, out = T.t[:, HC * i:HC * (i + 1)], T.h[:, i:4 * HC:P]
+            v.tensor_tensor(out, a, u(k), AluOpType.add).then_inc(T.sem.add, 1)
+    v.wait_ge(T.sem.add, (PER - 1) * P)
+    v.quantize_mx(T.qh[:], T.ph[:], T.h[:]).then_inc(T.sem.quh, 1)
+    g.wait_ge(T.sem.quh, 1)
+    moff, mon = _sum_masks(topo, summers, core, members[other][0], members[my][0])
+    for wch, ch, m in (("far", other, moff), ("own", my, mon)):
+        sem = T.sem["arrs_%s%d" % (wch, half)]
+        _send(g, T, topo, sent, [(_codes(T.qh[:]), [(c, _codes(_half(T["lqs_" + wch], half))) for c in members[ch]], m, sem)])
+        _send(g, T, topo, sent, [(T.ph[:], [(c, _half(T["lps_" + wch], half)) for c in members[ch]], m, sem)])
+    g.wait_ge(T.sem.sent, sent[0])
+
+
+def rank_program(g, core, T, topo):
+    plan = _plan(T, topo)
+    if T.rank_of(core) is not None:
+        _rank(g, core, T, topo, plan)
+    elif any(core in s for s in plan[3].values()):
+        _summer(g, core, T, topo, plan)

@@ -8,12 +8,16 @@ HC = NC // HALVES
 PER = 3
 P = 4
 MT = 128
+AH = P * MT // 2
+RUN = (MT, HC - MT)
 BANK = 512
+BANKS = 8
 SELW = 4 * MT + P - 1
+RELU, COPY = ActivationFunctionType.Relu, ActivationFunctionType.Copy
 
 SCRATCH = {
     "b_in": ("sbuf", [128, 4 * NC], "bfloat16"),
-    "a_in": ("sbuf", [128, 4 * 4 * MT], "bfloat16"),
+    "a_in": ("sbuf", [128, 4 * P * MT], "bfloat16"),
     "qb": ("sbuf", [128, NC], "float8_e4m3fn_x4"),
     "pb": ("sbuf", [128, NC], "uint8"),
     "qa": ("sbuf", [128, P * MT], "float8_e4m3fn_x4"),
@@ -23,25 +27,26 @@ SCRATCH = {
     "u": ("sbuf", [128, PER * P * HC], "bfloat16"),
     "t": ("sbuf", [128, P * HC], "bfloat16"),
     "h": ("sbuf", [128, 4 * HC], "bfloat16"),
-    "qh": ("sbuf", [128, HC], "float8_e4m3fn_x4"),
-    "ph": ("sbuf", [128, HC], "uint8"),
     "ones": ("sbuf", [128, SELW], "bfloat16"),
     "strip": ("sbuf", [128, SELW], "bfloat16"),
     "qw": ("sbuf", [128, P * MT], "float8_e4m3fn_x4"),
     "pw": ("sbuf", [128, P * MT], "uint8"),
     "yt": ("sbuf", [128, 4 * NC], "float32"),
-    "ps": ("psum", [128, BANK * 8], "float32"),
+    "ps": ("psum", [128, BANK * BANKS], "float32"),
 }
 for _k in range(PER):
     SCRATCH["lqa%d" % _k] = ("sbuf", [128, P * MT], "float8_e4m3fn_x4")
     SCRATCH["lpa%d" % _k] = ("sbuf", [128, P * MT], "uint8")
+for _k in range(2):
+    SCRATCH["qh%d" % _k] = ("sbuf", [128, MT], "float8_e4m3fn_x4")
+    SCRATCH["ph%d" % _k] = ("sbuf", [128, MT], "uint8")
 for _k in ("own", "far"):
     SCRATCH["lqs_" + _k] = ("sbuf", [128, NC], "float8_e4m3fn_x4")
     SCRATCH["lps_" + _k] = ("sbuf", [128, NC], "uint8")
 
-SEMAPHORES = (["ldb0", "ldb1", "lda0", "lda1", "qub", "qua", "one", "strip", "sel", "sent", "arrb", "mm", "rls", "rlv", "add", "quh",
+SEMAPHORES = (["ldb0", "ldb1", "lda0", "lda1", "qub", "qua", "one", "strip", "sel", "sent", "arrb", "pass", "mm", "rls", "rlv", "add", "quh",
                "mmy", "yv", "ys", "st"] + ["arra%d" % k for k in range(PER)]
-              + ["arrs_%s%d" % (w, h) for w in ("own", "far") for h in range(HALVES)])
+              + ["arrs_%s%d%d" % (w, h, n) for w in ("own", "far") for h in range(HALVES) for n in range(2)])
 
 
 def _engines(mask):
@@ -50,6 +55,10 @@ def _engines(mask):
 
 def _mask(engines):
     return sum(1 << e for e in engines)
+
+
+def _count(mask):
+    return len(_engines(mask))
 
 
 def _plan(T, topo):
@@ -64,166 +73,202 @@ def _plan(T, topo):
             if topo.chip(c) == ch and T.rank_of(c) is None and all(topo.may_write(c, f) for f in far):
                 by_die.setdefault(topo.die(c), c)
         summers[ch] = [by_die[d] for d in sorted(by_die)]
-    return chips, root, members, summers
+    return {"chips": chips, "root": root, "members": members, "summers": summers}
 
 
-def _dst(topo, c):
-    rid, pid, _ = topo.addr(c)
-    return DstId(rid=rid, pnc=pid)
+def _other(plan, ch):
+    return [c for c in plan["chips"] if c != ch][0]
+
+
+def _sum_masks(topo, plan, s):
+    ch = topo.chip(s)
+    off = topo.mask(s, plan["members"][_other(plan, ch)][0])
+    return {"far": off, "own": topo.mask(s, [c for c in plan["members"][ch] if c != s][0]) & ~off}
+
+
+def _halves(mask):
+    e = _engines(mask)
+    return [_mask(e[:len(e) // 2]), _mask(e[len(e) // 2:])]
 
 
 def _send(g, T, topo, sent, parts):
+    def dst(c):
+        rid, pid, _ = topo.addr(c)
+        return DstId(rid=rid, pnc=pid)
     g.remote_dma_fused(
-        [RemoteDMATransfer(dst_ids=[_dst(topo, c) for c, _ in dsts], dma_engine_mask=m, remote_sem=sem, srcs=[src], dsts=[d for _, d in dsts])
+        [RemoteDMATransfer(dst_ids=[dst(c) for c, _ in dsts], dma_engine_mask=m, remote_sem=sem, srcs=[src], dsts=[d for _, d in dsts])
          for src, dsts, m, sem in parts], local_sem=T.sem.sent)
-    sent[0] += sum(len(_engines(m)) for _, _, m, _ in parts)
+    sent[0] += sum(_count(m) for _, _, m, _ in parts)
 
 
 def _codes(view):
     return view.bitcast(dt.uint8)
 
 
-def _half(t, h):
-    return t[:, HC * h:HC * (h + 1)]
+def _cols(t, a, n, k=1):
+    return t[:, k * a:k * (a + n)]
+
+
+def _first(half, run):
+    return {(0, 0): 0, (0, 1): RUN[0], (1, 0): NC - RUN[0], (1, 1): HC}[half, run]
 
 
 def _rank(g, core, T, topo, plan):
-    chips, root, members, summers = plan
-    my = topo.chip(core)
-    is_root = core == root
+    my, root = topo.chip(core), plan["root"]
+    mine = plan["summers"][my]
     sent = [0]
+    v, te, sc = g.vector, g.tensor, g.scalar
     queues = (g.sync, g.scalar)
-    if is_root:
+    if core == root:
         for h in range(HALVES):
-            queues[h].dma_start(T.b_in[:, 4 * HC * h:4 * HC * (h + 1)], T.b[:, 4 * HC * h:4 * HC * (h + 1)]).then_inc(T.sem["ldb%d" % h], 16)
-    w = 2 * 4 * MT
+            queues[h].dma_start(_cols(T.b_in, HC * h, HC, 4), _cols(T.b, HC * h, HC, 4)).then_inc(T.sem["ldb%d" % h], 16)
     for h in range(2):
-        queues[h].dma_start(T.a_in[:, w * h:w * (h + 1)], T.a[:, w * h:w * (h + 1)]).then_inc(T.sem["lda%d" % h], 16)
-    v = g.vector
+        queues[h].dma_start(_cols(T.a_in, AH * h, AH, 4), _cols(T.a, AH * h, AH, 4)).then_inc(T.sem["lda%d" % h], 16)
     v.memset(T.ones[:], 1.0).then_inc(T.sem.one, 1)
-    if is_root:
+    if core == root:
         for h in range(HALVES):
             v.wait_ge(T.sem["ldb%d" % h], 16)
-            v.quantize_mx(_half(T.qb, h), _half(T.pb, h), T.b_in[:, 4 * HC * h:4 * HC * (h + 1)]).then_inc(T.sem.qub, 1)
+            v.quantize_mx(_cols(T.qb, HC * h, HC), _cols(T.pb, HC * h, HC), _cols(T.b_in, HC * h, HC, 4)).then_inc(T.sem.qub, 1)
     for h in range(2):
         v.wait_ge(T.sem["lda%d" % h], 16)
-        v.quantize_mx(T.qa[:, 2 * MT * h:2 * MT * (h + 1)], T.pa[:, 2 * MT * h:2 * MT * (h + 1)], T.a_in[:, w * h:w * (h + 1)]).then_inc(T.sem.qua, 1)
-    mine = summers[my]
+        v.quantize_mx(_cols(T.qa, AH * h, AH), _cols(T.pa, AH * h, AH), _cols(T.a_in, AH * h, AH, 4)).then_inc(T.sem.qua, 1)
+    if core == root:
+        masks = _sum_masks(topo, plan, core)
+        ways = [(plan["summers"][_other(plan, my)], masks["far"]), (mine, masks["own"])]
+        for h in range(HALVES):
+            g.wait_ge(T.sem.qub, h + 1)
+            _send(g, T, topo, sent, [(_codes(_cols(T.qb, HC * h, HC)), [(to[h], _codes(T.lqb[:]))], m, T.sem.arrb) for to, m in ways])
+        _send(g, T, topo, sent, [(_cols(T.pb, HC * h, HC), [(to[h], T.lpb[:])], _halves(m)[h], T.sem.arrb)
+                                 for to, m in ways for h in range(HALVES)])
     on = topo.mask(core, mine[0])
-    if is_root:
-        g.wait_ge(T.sem.qub, HALVES)
-        order = [ch for ch in chips if ch != my] + [my]
-        off = topo.mask(core, summers[order[0]][0])
-        for ch in order:
-            eng = _engines(off if ch != my else on & ~off)
-            k = len(eng) // HALVES
-            ms = [_mask(eng[k * h:k * (h + 1)]) for h in range(HALVES)]
-            for src, dst, f in ((T.qb, T.lqb, _codes), (T.pb, T.lpb, lambda x: x)):
-                _send(g, T, topo, sent, [(f(_half(src, h)), [(summers[ch][h], f(dst[:]))], ms[h], T.sem.arrb) for h in range(HALVES)])
+    k = plan["members"][my].index(core)
+    sem = T.sem["arra%d" % k]
+    qa, pa = T["lqa%d" % k], T["lpa%d" % k]
+    early = k < HALVES
+    g.wait_ge(T.sem.qua, 1)
+    if early:
+        _send(g, T, topo, sent, [(_cols(T.pa, 0, AH), [(mine[k], _cols(pa, 0, AH))], on, T.sem["pass"])])
+    _send(g, T, topo, sent, [(_codes(_cols(T.qa, 0, AH)), [(c, _codes(_cols(qa, 0, AH))) for c in mine], on, sem)])
     g.wait_ge(T.sem.qua, 2)
-    k = members[my].index(core)
-    _send(g, T, topo, sent, [(_codes(T.qa[:]), [(c, _codes(T["lqa%d" % k][:])) for c in mine], on, T.sem["arra%d" % k])])
-    _send(g, T, topo, sent, [(T.pa[:], [(c, T["lpa%d" % k][:]) for c in mine], on, T.sem["arra%d" % k])])
+    rest = (AH, AH) if early else (0, 2 * AH)
+    _send(g, T, topo, sent, [(_cols(T.pa, *rest), [(c, _cols(pa, *rest)) for c in mine], on, sem)])
+    _send(g, T, topo, sent, [(_codes(_cols(T.qa, AH, AH)), [(c, _codes(_cols(qa, AH, AH))) for c in mine], on, sem)])
     g.wait_ge(T.sem.one, 1)
     g.affine_select(T.strip[:], T.ones[:], [[1, SELW]], AluOpType.is_equal, 0.0, -(P - 1), -P).then_inc(T.sem.strip, 1)
     v.wait_ge(T.sem.strip, 1)
     for b in range(P):
-        v.quantize_mx(T.qw[:, MT * b:MT * (b + 1)], T.pw[:, MT * b:MT * (b + 1)], T.strip[:, P - 1 - b:P - 1 - b + 4 * MT]).then_inc(T.sem.sel, 1)
-    te = g.tensor
-    te.wait_ge(T.sem.sel, P)
-    for wch, first in (("own", True), ("far", False)):
-        for h in range(HALVES):
-            te.wait_ge(T.sem["arrs_%s%d" % (wch, h)], _sum_count(topo, summers, my, wch, core, h))
-            for b in range(P):
-                bank = P * h + b
-                m = te.matmul_mx(T.ps[:, BANK * bank:BANK * bank + HC], T.qw[:, MT * b:MT * (b + 1)], T.pw[:, MT * b:MT * (b + 1)],
-                                 _half(T["lqs_" + wch], h), _half(T["lps_" + wch], h), first, not first)
-                if not first:
-                    m.then_inc(T.sem.mmy, 1)
-    for h in range(HALVES):
+        v.quantize_mx(_cols(T.qw, MT * b, MT), _cols(T.pw, MT * b, MT), T.strip[:, P - 1 - b:P - 1 - b + 4 * MT]).then_inc(T.sem.sel, 1)
+    blocks = ((0, 0, ((0, 0),)), (2 * MT, P, ((1, 0),)), (MT, 0, ((0, 1), (1, 1))))
+
+    def unpack(n, wch):
+        c0, bank, runs = blocks[n]
+        for half, run in runs:
+            s = plan["summers"][my if wch == "own" else _other(plan, my)][half]
+            te.wait_ge(T.sem["arrs_%s%d%d" % (wch, half, run)], 2 * _count(_sum_masks(topo, plan, s)[wch]))
         for b in range(P):
-            bank = P * h + b
-            src = T.ps[:, BANK * bank:BANK * bank + HC]
-            out = T.yt[:, 4 * HC * h + b:4 * HC * (h + 1):P]
+            m = te.matmul_mx(T.ps[:, BANK * (bank + b):BANK * (bank + b) + MT], _cols(T.qw, MT * b, MT), _cols(T.pw, MT * b, MT),
+                             _cols(T["lqs_" + wch], c0, MT), _cols(T["lps_" + wch], c0, MT), wch == "own", wch == "far")
+            if wch == "far":
+                m.then_inc(T.sem.mmy, 1)
+    te.wait_ge(T.sem.sel, P)
+    unpack(0, "own")
+    unpack(1, "own")
+    unpack(0, "far")
+    unpack(1, "far")
+    te.wait_ge(T.sem.ys, P // 2)
+    te.wait_ge(T.sem.yv, P // 2)
+    unpack(2, "own")
+    unpack(2, "far")
+    for n, (c0, bank, _) in enumerate(blocks):
+        for b in range(P):
+            src = T.ps[:, BANK * (bank + b):BANK * (bank + b) + MT]
+            out = T.yt[:, 4 * c0 + b:4 * (c0 + MT):P]
             if b % 2 == 0:
-                g.scalar.wait_ge(T.sem.mmy, bank + 1)
-                g.scalar.activation(out, src, ActivationFunctionType.Copy).then_inc(T.sem.ys, 1)
+                sc.wait_ge(T.sem.mmy, P * n + b + 1)
+                sc.activation(out, src, COPY).then_inc(T.sem.ys, 1)
             else:
-                v.wait_ge(T.sem.mmy, bank + 1)
+                v.wait_ge(T.sem.mmy, P * n + b + 1)
                 v.tensor_copy(out, src).then_inc(T.sem.yv, 1)
-        g.sync.wait_ge(T.sem.ys, (P // 2) * (h + 1))
-        g.sync.wait_ge(T.sem.yv, (P // 2) * (h + 1))
-        g.sync.dma_start(T.y[:, 4 * HC * h:4 * HC * (h + 1)], T.yt[:, 4 * HC * h:4 * HC * (h + 1)]).then_inc(T.sem.st, 16)
-    g.sync.wait_ge(T.sem.st, 16 * HALVES)
+        g.sync.wait_ge(T.sem.ys, (P // 2) * (n + 1))
+        g.sync.wait_ge(T.sem.yv, (P // 2) * (n + 1))
+        g.sync.dma_start(_cols(T.y, c0, MT, 4), _cols(T.yt, c0, MT, 4)).then_inc(T.sem.st, 16)
+    g.sync.wait_ge(T.sem.st, 16 * len(blocks))
     g.wait_ge(T.sem.sent, sent[0])
 
 
-def _sum_masks(topo, summers, core, far_core, near_core):
-    off = topo.mask(core, far_core)
-    return off, topo.mask(core, near_core) & ~off
-
-
-def _sum_count(topo, summers, my, wch, core, h):
-    other = [ch for ch in summers if ch != my][0]
-    if wch == "own":
-        s = summers[my][h]
-        off, on = _sum_masks(topo, summers, s, summers[other][h], core)
-        return 2 * len(_engines(on))
-    return 2 * len(_engines(topo.mask(summers[other][h], core)))
-
-
 def _summer(g, core, T, topo, plan):
-    chips, root, members, summers = plan
     my = topo.chip(core)
-    other = [ch for ch in chips if ch != my][0]
-    half = summers[my].index(core)
-    rchip = topo.chip(root)
+    other = _other(plan, my)
+    members, root = plan["members"], plan["root"]
+    half = plan["summers"][my].index(core)
+    peer = plan["summers"][my][1 - half]
+    on = topo.mask(core, peer)
     sent = [0]
     te, v, sc = g.tensor, g.vector, g.scalar
-    off = topo.mask(root, summers[[ch for ch in chips if ch != rchip][0]][0])
-    nb = len(_engines(off if my != rchip else topo.mask(root, core) & ~off)) // HALVES
-    on_vec = [k for k in range(PER * P) if k in (1, 3)]
-    def clamped_before(k, vec):
+    g.wait_ge(T.sem["pass"], _count(topo.mask(members[my][half], core)))
+    mine = _cols(T["lpa%d" % half], 0, AH)
+    _send(g, T, topo, sent, [(mine, [(peer, mine)], on, T.sem["arra%d" % half])])
+    late = PER - 1 if root in members[my] else 1 - half
+    order = [half] + [r for r in range(PER) if r not in (half, late)] + [late]
+    bm = _sum_masks(topo, plan, root)["own" if root in members[my] else "far"]
+    te.wait_ge(T.sem.arrb, _count(bm) + _count(_halves(bm)[half]))
+    base = HC * half
+    todo = [(n, o, i) for n in range(2) for o in range(PER) for i in range(P)]
+    on_vec = [k for k, (n, o, i) in enumerate(todo) if (n, o) == (0, 0) and i % 2 == 1]
+    first = [_first(half, n) - base for n in range(2)]
+    win = [first[0], 0 if half else HC - MT]
+
+    def before(k, vec):
         return len([j for j in range(k) if (j in on_vec) == vec])
-    def z(k):
-        return T.ps[:, BANK * (k % 8):BANK * (k % 8) + HC]
-    def u(k):
-        return T.u[:, HC * k:HC * (k + 1)]
-    te.wait_ge(T.sem.arrb, 2 * nb)
-    for k in range(PER * P):
-        r, i = divmod(k, P)
-        if i == 0:
-            te.wait_ge(T.sem["arra%d" % r], 2 * len(_engines(topo.mask(members[my][r], core))))
-        if k >= 8:
-            j = k - 8
-            te.wait_ge(T.sem.rlv if j in on_vec else T.sem.rls, clamped_before(j + 1, j in on_vec))
-        te.matmul_mx(z(k), T["lqa%d" % r][:, MT * i:MT * (i + 1)], T["lpa%d" % r][:, MT * i:MT * (i + 1)], T.lqb[:], T.lpb[:], True, True).then_inc(T.sem.mm, 1)
-    for k in range(PER * P):
+
+    def z(k, n, own):
+        c = first[n] - win[n] if own else 0
+        return T.ps[:, BANK * (k % BANKS) + c:BANK * (k % BANKS) + c + (RUN[n] if own else MT)]
+
+    def u(n, o, i):
+        return _cols(T.u, HC * (P * o + i) + first[n], RUN[n])
+    for k, (n, o, i) in enumerate(todo):
+        r = order[o]
+        if n == 0 and i == 0:
+            c = 3 * _count(topo.mask(members[my][r], core))
+            if r == half:
+                te.wait_ge(T.sem["pass"], _count(topo.mask(members[my][r], core)))
+            elif r < HALVES:
+                c += _count(topo.mask(peer, core))
+            te.wait_ge(T.sem["arra%d" % r], c)
+        if k >= BANKS:
+            j = k - BANKS
+            te.wait_ge(T.sem.rlv if j in on_vec else T.sem.rls, before(j + 1, j in on_vec))
+        te.matmul_mx(z(k, n, False), _cols(T["lqa%d" % r], MT * i, MT), _cols(T["lpa%d" % r], MT * i, MT),
+                     _cols(T.lqb, win[n], MT), _cols(T.lpb, win[n], MT), True, True).then_inc(T.sem.mm, 1)
+    for k, (n, o, i) in enumerate(todo):
         if k in on_vec:
             v.wait_ge(T.sem.mm, k + 1)
-            v.tensor_scalar(u(k), z(k), 0.0, None, AluOpType.max).then_inc(T.sem.rlv, 1)
+            v.tensor_scalar(u(n, o, i), z(k, n, True), 0.0, None, AluOpType.max).then_inc(T.sem.rlv, 1)
         else:
             sc.wait_ge(T.sem.mm, k + 1)
-            sc.activation(u(k), z(k), ActivationFunctionType.Relu).then_inc(T.sem.rls, 1)
+            sc.activation(u(n, o, i), z(k, n, True), RELU).then_inc(T.sem.rls, 1)
     v.wait_ge(T.sem.rlv, len(on_vec))
-    for r in range(1, PER):
-        for i in range(P):
-            k = P * r + i
-            v.wait_ge(T.sem.rls, clamped_before(k + 1, False))
-            if r == 1:
-                a, out = u(i), T.t[:, HC * i:HC * (i + 1)]
-            else:
-                v.wait_ge(T.sem.add, i + 1)
-                a, out = T.t[:, HC * i:HC * (i + 1)], T.h[:, i:4 * HC:P]
-            v.tensor_tensor(out, a, u(k), AluOpType.add).then_inc(T.sem.add, 1)
-    v.wait_ge(T.sem.add, (PER - 1) * P)
-    v.quantize_mx(T.qh[:], T.ph[:], T.h[:]).then_inc(T.sem.quh, 1)
-    g.wait_ge(T.sem.quh, 1)
-    moff, mon = _sum_masks(topo, summers, core, members[other][0], members[my][0])
-    for wch, ch, m in (("far", other, moff), ("own", my, mon)):
-        sem = T.sem["arrs_%s%d" % (wch, half)]
-        _send(g, T, topo, sent, [(_codes(T.qh[:]), [(c, _codes(_half(T["lqs_" + wch], half))) for c in members[ch]], m, sem)])
-        _send(g, T, topo, sent, [(T.ph[:], [(c, _half(T["lps_" + wch], half)) for c in members[ch]], m, sem)])
+    adds = 0
+    for n in range(2):
+        for o in range(1, PER):
+            for i in range(P):
+                v.wait_ge(T.sem.rls, before(P * (PER * n + o) + i + 1, False))
+                if o > 1:
+                    v.wait_ge(T.sem.add, adds - P + 1)
+                t = _cols(T.t, HC * i + first[n], RUN[n])
+                out = t if o < PER - 1 else T.h[:, 4 * first[n] + i:4 * (first[n] + RUN[n]):P]
+                v.tensor_tensor(out, u(n, 0, i) if o == 1 else t, u(n, o, i), AluOpType.add).then_inc(T.sem.add, 1)
+                adds += 1
+        v.wait_ge(T.sem.add, adds)
+        v.quantize_mx(T["qh%d" % n][:], T["ph%d" % n][:], _cols(T.h, win[n], MT, 4)).then_inc(T.sem.quh, 1)
+    masks = _sum_masks(topo, plan, core)
+    for n in range(2):
+        g.wait_ge(T.sem.quh, n + 1)
+        c, c0 = first[n] - win[n], _first(half, n)
+        for src, land, f in ((T["qh%d" % n], "lqs_", _codes), (T["ph%d" % n], "lps_", lambda x: x)):
+            _send(g, T, topo, sent, [(f(_cols(src, c, RUN[n])), [(d, f(_cols(T[land + wch], c0, RUN[n]))) for d in members[ch]],
+                                      masks[wch], T.sem["arrs_%s%d%d" % (wch, half, n)]) for wch, ch in (("far", other), ("own", my))])
     g.wait_ge(T.sem.sent, sent[0])
 
 
@@ -231,5 +276,5 @@ def rank_program(g, core, T, topo):
     plan = _plan(T, topo)
     if T.rank_of(core) is not None:
         _rank(g, core, T, topo, plan)
-    elif any(core in s for s in plan[3].values()):
+    elif any(core in s for s in plan["summers"].values()):
         _summer(g, core, T, topo, plan)

from concourse.bass import DstId, RemoteDMATransfer
from concourse.mybir import dt, AluOpType, ActivationFunctionType

SIM_CORES = 16
NC = 384
HALVES = 2
HC = NC // HALVES
PER = 3
P = 4
MT = 128
AH = P * MT // 2
RUN = (MT, HC - MT)
BANK = 512
BANKS = 8
SELW = 4 * MT + P - 1
RELU, COPY = ActivationFunctionType.Relu, ActivationFunctionType.Copy

SCRATCH = {
    "b_in": ("sbuf", [128, 4 * NC], "bfloat16"),
    "a_in": ("sbuf", [128, 4 * P * MT], "bfloat16"),
    "qb": ("sbuf", [128, NC], "float8_e4m3fn_x4"),
    "pb": ("sbuf", [128, NC], "uint8"),
    "qa": ("sbuf", [128, P * MT], "float8_e4m3fn_x4"),
    "pa": ("sbuf", [128, P * MT], "uint8"),
    "lqb": ("sbuf", [128, HC], "float8_e4m3fn_x4"),
    "lpb": ("sbuf", [128, HC], "uint8"),
    "u": ("sbuf", [128, PER * P * HC], "bfloat16"),
    "t": ("sbuf", [128, P * HC], "bfloat16"),
    "h": ("sbuf", [128, 4 * HC], "bfloat16"),
    "ones": ("sbuf", [128, SELW], "bfloat16"),
    "strip": ("sbuf", [128, SELW], "bfloat16"),
    "qw": ("sbuf", [128, P * MT], "float8_e4m3fn_x4"),
    "pw": ("sbuf", [128, P * MT], "uint8"),
    "yt": ("sbuf", [128, 4 * NC], "float32"),
    "ps": ("psum", [128, BANK * BANKS], "float32"),
}
for _k in range(PER):
    SCRATCH["lqa%d" % _k] = ("sbuf", [128, P * MT], "float8_e4m3fn_x4")
    SCRATCH["lpa%d" % _k] = ("sbuf", [128, P * MT], "uint8")
for _k in range(2):
    SCRATCH["qh%d" % _k] = ("sbuf", [128, MT], "float8_e4m3fn_x4")
    SCRATCH["ph%d" % _k] = ("sbuf", [128, MT], "uint8")
for _k in ("own", "far"):
    SCRATCH["lqs_" + _k] = ("sbuf", [128, NC], "float8_e4m3fn_x4")
    SCRATCH["lps_" + _k] = ("sbuf", [128, NC], "uint8")

SEMAPHORES = (["ldb0", "ldb1", "lda0", "lda1", "qub", "qua", "one", "strip", "sel", "sent", "arrb", "pass", "mm", "rls", "rlv", "add", "quh",
               "mmy", "yv", "ys", "st"] + ["arra%d" % k for k in range(PER)]
              + ["arrs_%s%d%d" % (w, h, n) for w in ("own", "far") for h in range(HALVES) for n in range(2)])


def _engines(mask):
    return [e for e in range(mask.bit_length()) if mask >> e & 1]


def _mask(engines):
    return sum(1 << e for e in engines)


def _count(mask):
    return len(_engines(mask))


def _plan(T, topo):
    chips = sorted({topo.chip(c) for c in T.cores})
    root = T.cores[T.root]
    members = {ch: sorted([c for c in T.cores if topo.chip(c) == ch], key=lambda c: (c == root, c)) for ch in chips}
    summers = {}
    for ch in chips:
        far = [c for c in T.cores if topo.chip(c) != ch]
        by_die = {}
        for c in range(SIM_CORES):
            if topo.chip(c) == ch and T.rank_of(c) is None and all(topo.may_write(c, f) for f in far):
                by_die.setdefault(topo.die(c), c)
        summers[ch] = [by_die[d] for d in sorted(by_die)]
    return {"chips": chips, "root": root, "members": members, "summers": summers}


def _other(plan, ch):
    return [c for c in plan["chips"] if c != ch][0]


def _sum_masks(topo, plan, s):
    ch = topo.chip(s)
    off = topo.mask(s, plan["members"][_other(plan, ch)][0])
    return {"far": off, "own": topo.mask(s, [c for c in plan["members"][ch] if c != s][0]) & ~off}


def _halves(mask):
    e = _engines(mask)
    return [_mask(e[:len(e) // 2]), _mask(e[len(e) // 2:])]


def _send(g, T, topo, sent, parts):
    def dst(c):
        rid, pid, _ = topo.addr(c)
        return DstId(rid=rid, pnc=pid)
    g.remote_dma_fused(
        [RemoteDMATransfer(dst_ids=[dst(c) for c, _ in dsts], dma_engine_mask=m, remote_sem=sem, srcs=[src], dsts=[d for _, d in dsts])
         for src, dsts, m, sem in parts], local_sem=T.sem.sent)
    sent[0] += sum(_count(m) for _, _, m, _ in parts)


def _codes(view):
    return view.bitcast(dt.uint8)


def _cols(t, a, n, k=1):
    return t[:, k * a:k * (a + n)]


def _first(half, run):
    return {(0, 0): 0, (0, 1): RUN[0], (1, 0): NC - RUN[0], (1, 1): HC}[half, run]


def _rank(g, core, T, topo, plan):
    my, root = topo.chip(core), plan["root"]
    mine = plan["summers"][my]
    sent = [0]
    v, te, sc = g.vector, g.tensor, g.scalar
    queues = (g.sync, g.scalar)
    if core == root:
        for h in range(HALVES):
            queues[h].dma_start(_cols(T.b_in, HC * h, HC, 4), _cols(T.b, HC * h, HC, 4)).then_inc(T.sem["ldb%d" % h], 16)
    for h in range(2):
        queues[h].dma_start(_cols(T.a_in, AH * h, AH, 4), _cols(T.a, AH * h, AH, 4)).then_inc(T.sem["lda%d" % h], 16)
    v.memset(T.ones[:], 1.0).then_inc(T.sem.one, 1)
    if core == root:
        for h in range(HALVES):
            v.wait_ge(T.sem["ldb%d" % h], 16)
            v.quantize_mx(_cols(T.qb, HC * h, HC), _cols(T.pb, HC * h, HC), _cols(T.b_in, HC * h, HC, 4)).then_inc(T.sem.qub, 1)
    for h in range(2):
        v.wait_ge(T.sem["lda%d" % h], 16)
        v.quantize_mx(_cols(T.qa, AH * h, AH), _cols(T.pa, AH * h, AH), _cols(T.a_in, AH * h, AH, 4)).then_inc(T.sem.qua, 1)
    if core == root:
        masks = _sum_masks(topo, plan, core)
        ways = [(plan["summers"][_other(plan, my)], masks["far"]), (mine, masks["own"])]
        for h in range(HALVES):
            g.wait_ge(T.sem.qub, h + 1)
            _send(g, T, topo, sent, [(_codes(_cols(T.qb, HC * h, HC)), [(to[h], _codes(T.lqb[:]))], m, T.sem.arrb) for to, m in ways])
        _send(g, T, topo, sent, [(_cols(T.pb, HC * h, HC), [(to[h], T.lpb[:])], _halves(m)[h], T.sem.arrb)
                                 for to, m in ways for h in range(HALVES)])
    on = topo.mask(core, mine[0])
    k = plan["members"][my].index(core)
    sem = T.sem["arra%d" % k]
    qa, pa = T["lqa%d" % k], T["lpa%d" % k]
    early = k < HALVES
    g.wait_ge(T.sem.qua, 1)
    if early:
        _send(g, T, topo, sent, [(_cols(T.pa, 0, AH), [(mine[k], _cols(pa, 0, AH))], on, T.sem["pass"])])
    _send(g, T, topo, sent, [(_codes(_cols(T.qa, 0, AH)), [(c, _codes(_cols(qa, 0, AH))) for c in mine], on, sem)])
    g.wait_ge(T.sem.qua, 2)
    rest = (AH, AH) if early else (0, 2 * AH)
    _send(g, T, topo, sent, [(_cols(T.pa, *rest), [(c, _cols(pa, *rest)) for c in mine], on, sem)])
    _send(g, T, topo, sent, [(_codes(_cols(T.qa, AH, AH)), [(c, _codes(_cols(qa, AH, AH))) for c in mine], on, sem)])
    g.wait_ge(T.sem.one, 1)
    g.affine_select(T.strip[:], T.ones[:], [[1, SELW]], AluOpType.is_equal, 0.0, -(P - 1), -P).then_inc(T.sem.strip, 1)
    v.wait_ge(T.sem.strip, 1)
    for b in range(P):
        v.quantize_mx(_cols(T.qw, MT * b, MT), _cols(T.pw, MT * b, MT), T.strip[:, P - 1 - b:P - 1 - b + 4 * MT]).then_inc(T.sem.sel, 1)
    blocks = ((0, 0, ((0, 0),)), (2 * MT, P, ((1, 0),)), (MT, 0, ((0, 1), (1, 1))))

    def unpack(n, wch):
        c0, bank, runs = blocks[n]
        for half, run in runs:
            s = plan["summers"][my if wch == "own" else _other(plan, my)][half]
            te.wait_ge(T.sem["arrs_%s%d%d" % (wch, half, run)], 2 * _count(_sum_masks(topo, plan, s)[wch]))
        for b in range(P):
            m = te.matmul_mx(T.ps[:, BANK * (bank + b):BANK * (bank + b) + MT], _cols(T.qw, MT * b, MT), _cols(T.pw, MT * b, MT),
                             _cols(T["lqs_" + wch], c0, MT), _cols(T["lps_" + wch], c0, MT), wch == "own", wch == "far")
            if wch == "far":
                m.then_inc(T.sem.mmy, 1)
    te.wait_ge(T.sem.sel, P)
    unpack(0, "own")
    unpack(1, "own")
    unpack(0, "far")
    unpack(1, "far")
    te.wait_ge(T.sem.ys, P // 2)
    te.wait_ge(T.sem.yv, P // 2)
    unpack(2, "own")
    unpack(2, "far")
    for n, (c0, bank, _) in enumerate(blocks):
        for b in range(P):
            src = T.ps[:, BANK * (bank + b):BANK * (bank + b) + MT]
            out = T.yt[:, 4 * c0 + b:4 * (c0 + MT):P]
            if b % 2 == 0:
                sc.wait_ge(T.sem.mmy, P * n + b + 1)
                sc.activation(out, src, COPY).then_inc(T.sem.ys, 1)
            else:
                v.wait_ge(T.sem.mmy, P * n + b + 1)
                v.tensor_copy(out, src).then_inc(T.sem.yv, 1)
        g.sync.wait_ge(T.sem.ys, (P // 2) * (n + 1))
        g.sync.wait_ge(T.sem.yv, (P // 2) * (n + 1))
        g.sync.dma_start(_cols(T.y, c0, MT, 4), _cols(T.yt, c0, MT, 4)).then_inc(T.sem.st, 16)
    g.sync.wait_ge(T.sem.st, 16 * len(blocks))
    g.wait_ge(T.sem.sent, sent[0])


def _summer(g, core, T, topo, plan):
    my = topo.chip(core)
    other = _other(plan, my)
    members, root = plan["members"], plan["root"]
    half = plan["summers"][my].index(core)
    peer = plan["summers"][my][1 - half]
    on = topo.mask(core, peer)
    sent = [0]
    te, v, sc = g.tensor, g.vector, g.scalar
    g.wait_ge(T.sem["pass"], _count(topo.mask(members[my][half], core)))
    mine = _cols(T["lpa%d" % half], 0, AH)
    _send(g, T, topo, sent, [(mine, [(peer, mine)], on, T.sem["arra%d" % half])])
    late = PER - 1 if root in members[my] else 1 - half
    order = [half] + [r for r in range(PER) if r not in (half, late)] + [late]
    bm = _sum_masks(topo, plan, root)["own" if root in members[my] else "far"]
    te.wait_ge(T.sem.arrb, _count(bm) + _count(_halves(bm)[half]))
    base = HC * half
    todo = [(n, o, i) for n in range(2) for o in range(PER) for i in range(P)]
    on_vec = [k for k, (n, o, i) in enumerate(todo) if (n, o) == (0, 0) and i % 2 == 1]
    first = [_first(half, n) - base for n in range(2)]
    win = [first[0], 0 if half else HC - MT]

    def before(k, vec):
        return len([j for j in range(k) if (j in on_vec) == vec])

    def z(k, n, own):
        c = first[n] - win[n] if own else 0
        return T.ps[:, BANK * (k % BANKS) + c:BANK * (k % BANKS) + c + (RUN[n] if own else MT)]

    def u(n, o, i):
        return _cols(T.u, HC * (P * o + i) + first[n], RUN[n])
    for k, (n, o, i) in enumerate(todo):
        r = order[o]
        if n == 0 and i == 0:
            c = 3 * _count(topo.mask(members[my][r], core))
            if r == half:
                te.wait_ge(T.sem["pass"], _count(topo.mask(members[my][r], core)))
            elif r < HALVES:
                c += _count(topo.mask(peer, core))
            te.wait_ge(T.sem["arra%d" % r], c)
        if k >= BANKS:
            j = k - BANKS
            te.wait_ge(T.sem.rlv if j in on_vec else T.sem.rls, before(j + 1, j in on_vec))
        te.matmul_mx(z(k, n, False), _cols(T["lqa%d" % r], MT * i, MT), _cols(T["lpa%d" % r], MT * i, MT),
                     _cols(T.lqb, win[n], MT), _cols(T.lpb, win[n], MT), True, True).then_inc(T.sem.mm, 1)
    for k, (n, o, i) in enumerate(todo):
        if k in on_vec:
            v.wait_ge(T.sem.mm, k + 1)
            v.tensor_scalar(u(n, o, i), z(k, n, True), 0.0, None, AluOpType.max).then_inc(T.sem.rlv, 1)
        else:
            sc.wait_ge(T.sem.mm, k + 1)
            sc.activation(u(n, o, i), z(k, n, True), RELU).then_inc(T.sem.rls, 1)
    v.wait_ge(T.sem.rlv, len(on_vec))
    adds = 0
    for n in range(2):
        for o in range(1, PER):
            for i in range(P):
                v.wait_ge(T.sem.rls, before(P * (PER * n + o) + i + 1, False))
                if o > 1:
                    v.wait_ge(T.sem.add, adds - P + 1)
                t = _cols(T.t, HC * i + first[n], RUN[n])
                out = t if o < PER - 1 else T.h[:, 4 * first[n] + i:4 * (first[n] + RUN[n]):P]
                v.tensor_tensor(out, u(n, 0, i) if o == 1 else t, u(n, o, i), AluOpType.add).then_inc(T.sem.add, 1)
                adds += 1
        v.wait_ge(T.sem.add, adds)
        v.quantize_mx(T["qh%d" % n][:], T["ph%d" % n][:], _cols(T.h, win[n], MT, 4)).then_inc(T.sem.quh, 1)
    masks = _sum_masks(topo, plan, core)
    for n in range(2):
        g.wait_ge(T.sem.quh, n + 1)
        c, c0 = first[n] - win[n], _first(half, n)
        for src, land, f in ((T["qh%d" % n], "lqs_", _codes), (T["ph%d" % n], "lps_", lambda x: x)):
            _send(g, T, topo, sent, [(f(_cols(src, c, RUN[n])), [(d, f(_cols(T[land + wch], c0, RUN[n]))) for d in members[ch]],
                                      masks[wch], T.sem["arrs_%s%d%d" % (wch, half, n)]) for wch, ch in (("far", other), ("own", my))])
    g.wait_ge(T.sem.sent, sent[0])


def rank_program(g, core, T, topo):
    plan = _plan(T, topo)
    if T.rank_of(core) is not None:
        _rank(g, core, T, topo, plan)
    elif any(core in s for s in plan["summers"].values()):
        _summer(g, core, T, topo, plan)
